import numpy as np
import ml_dtypes


def mxq(x, axis, fmt="e4m3"):
    dtype, down = {"e4m3": (ml_dtypes.float8_e4m3fn, 7), "e5m2": (ml_dtypes.float8_e5m2, 14)}[fmt]
    v = np.moveaxis(np.asarray(x, np.float32).astype(ml_dtypes.bfloat16).astype(np.float64), axis, -1)
    blocks = v.reshape(v.shape[:-1] + (-1, 32))
    amax = np.abs(blocks).max(-1, keepdims=True)
    byte = np.maximum(np.where(amax > 0, np.frexp(amax)[1] - 1 + 127, 0) - down, 1)
    scale = np.exp2(byte - 127.0)
    codes = (blocks / scale).astype(np.float32).astype(dtype).astype(np.float64)
    return np.moveaxis((codes * scale).reshape(v.shape), -1, axis)


WIDE = False


def mx_kscale(k):
    if not WIDE:
        return np.ones(k)
    levels = np.array([10, -10, 5, -5, 0])
    if k % 512:
        return np.exp2(np.random.permutation(np.resize(levels, k // 32))).repeat(32)
    a = np.empty((k // 512, 16))
    for p in range(k // 512):
        a[p, :8] = np.random.permutation(np.resize(levels, 8))
        for g in range(8):
            far = levels[np.abs(levels - a[p, g]) >= 10]
            a[p, g + 8] = far[np.random.randint(len(far))]
    return np.exp2(a.ravel()).repeat(32)


BF16 = ml_dtypes.bfloat16


def bf(x):
    return np.asarray(x, np.float32).astype(BF16)


def f64(x):
    return np.asarray(x).astype(np.float64)

E4M3FN = np.array([(-1.0 if i & 128 else 1.0) * ((1.0 + (i & 7) / 8.0) * 2.0 ** (((i >> 3) & 15) - 7) if i & 120 else (i & 7) * 2.0 ** -9) for i in range(256)])


def e4m3fn_bytes(y):
    return np.clip(np.asarray(y, np.float64), -448.0, 448.0).astype(np.float32).astype(ml_dtypes.float8_e4m3fn).view(np.uint8)


def e4m3fn_values(b):
    return E4M3FN[b]


B, S, G = 1024, 2048, 128


def setup_inputs():
    s = mx_kscale(S)
    alpha = np.exp(1.5 * np.random.standard_normal((B, S)) - 1.125)
    trans = np.exp(1.5 * np.random.standard_normal((S, S)))
    trans = trans / trans.sum(axis=0, keepdims=True)
    trans = trans / s[None, :]
    top = np.abs(trans).reshape(S, S // G, G).max(axis=2)
    trans_scale = (top / 448.0).astype(np.float32)
    wide = np.repeat(f64(trans_scale), G, axis=1)
    return {"alpha": bf(alpha * s),
            "trans_bytes": e4m3fn_bytes(trans / wide),
            "trans_scale": trans_scale,
            "loglik": bf(0.5 * np.random.standard_normal((B, S)))}


def reference(alpha, trans_bytes, trans_scale, loglik):
    trans = e4m3fn_values(trans_bytes) * np.repeat(f64(trans_scale), G, axis=1)
    aq = mxq(f64(alpha), 1, "e4m3")
    tq = mxq(trans, 1, "e4m3")
    pred = aq @ tq.T
    forward = pred * np.exp(f64(loglik))
    return pred, forward

@@ -1,0 +1,237 @@
+from contextlib import ExitStack
+
+import concourse.mybir as mybir
+from concourse.masks import make_identity
+
+B, S = 1024, 2048
+P = 128
+FLOPS = 2 * B * S * S
+
+F32 = mybir.dt.float32
+BF16 = mybir.dt.bfloat16
+U32 = mybir.dt.uint32
+U8 = mybir.dt.uint8
+FP8 = mybir.dt.float8_e4m3fn
+FP8X4 = mybir.dt.float8_e4m3fn_x4
+MULT = mybir.AluOpType.mult
+EXP = mybir.ActivationFunctionType.Exp
+
+N_UNITS = 16
+N_ITEMS = 32
+
+
+def tile_hmm_forward_step_d1_kernel(tc, alpha, trans_bytes, trans_scale, loglik, out_0, out_1):
+    nc = tc.nc
+    bytes_view = trans_bytes.rearrange("(k p r) s -> k p r s", p=P, r=2)
+    scale_view = trans_scale.rearrange("(k p r) c -> p k (r c)", p=P, r=2)
+    loglik_view = loglik.rearrange("(b p) j -> p b j", p=P)
+    out_views = [o.rearrange("(b p) j -> p b j", p=P) for o in (out_0, out_1)]
+
+    with ExitStack() as ctx:
+        keep = ctx.enter_context(tc.tile_pool(name="keep", bufs=1))
+        work = ctx.enter_context(tc.tile_pool(name="work", bufs=3))
+        psum = ctx.enter_context(tc.psum_pool(name="psum", bufs=4))
+
+        ident = keep.tile([P, P], F32, name="ident")
+        make_identity(nc, ident[:])
+
+        ctx.enter_context(tc.manual_schedule())
+
+        scl = keep.tile([P, 256], F32, name="scl")
+        fp8_t = [keep.tile([P, 2, S], U8, name="fp8_%d" % k) for k in range(8)]
+        a_t = [keep.tile([P, S], BF16, name="a_%d" % b) for b in range(8)]
+        ll_t = [[keep.tile([P, 2, 1024], BF16, name="ll_%d_%d" % (h, bp)) for bp in range(4)] for h in range(2)]
+
+        def load_bytes(k, lo, hi):
+            nc.sync.dma_start(out=fp8_t[k][:, :, lo:hi], in_=bytes_view[k][:, :, lo:hi])
+
+        def load_alpha(b):
+            nc.sync.dma_start(out=a_t[b][:], in_=alpha[b * P:(b + 1) * P, :])
+
+        def load_ll(h, bp):
+            nc.sync.dma_start(out=ll_t[h][bp][:], in_=loglik_view[:, 2 * bp:2 * bp + 2, 1024 * h:1024 * (h + 1)])
+
+        nc.scalar.dma_start(out=scl[:].rearrange("p (k x) -> p k x", k=8), in_=scale_view)
+        load_bytes(0, 0, 1024)
+        load_bytes(0, 1024, 2048)
+        load_alpha(0)
+        load_alpha(1)
+        load_ll(0, 0)
+        load_alpha(2)
+        load_alpha(3)
+        load_bytes(1, 0, 2048)
+        load_ll(0, 1)
+        load_alpha(4)
+        load_alpha(5)
+        load_ll(0, 2)
+        load_alpha(6)
+        load_alpha(7)
+        load_bytes(2, 0, 2048)
+        load_ll(0, 3)
+        load_bytes(3, 0, 2048)
+        load_bytes(4, 0, 2048)
+        load_ll(1, 0)
+        load_ll(1, 1)
+        load_bytes(5, 0, 2048)
+        load_ll(1, 2)
+        load_ll(1, 3)
+        load_bytes(6, 0, 2048)
+        load_bytes(7, 0, 2048)
+
+        t_codes = [keep.tile([P, 512], U32, name="tc_%d" % n, align_bytes=64) for n in range(N_UNITS)]
+        t_scales = [keep.tile([P, 512], U8, name="ts_%d" % n, align_bytes=64) for n in range(N_UNITS)]
+        a_codes = [keep.tile([P, 512], U32, name="ac_%d" % b, align_bytes=64) for b in range(8)]
+        a_scales = [keep.tile([P, 512], U8, name="as_%d" % b, align_bytes=64) for b in range(8)]
+
+        wide_t = {}
+        t_group = {}
+        a_group = {}
+
+        def widen(n):
+            k, gh = n // 2, n % 2
+            w = work.tile([P, 2048], BF16, name="wide", bufs=2, align_bytes=64)
+            wide_t[n] = w
+            for gi in range(2):
+                for r in range(2):
+                    blk = 2 * gi + r
+                    dst = w[:, 512 * blk:512 * (blk + 1)].rearrange("j (u p e) -> j p u e", u=2, e=2)
+                    for q in range(4):
+                        c = 4 * (2 * gh + gi) + q
+                        col = 32 * k + 16 * r + c
+                        src = fp8_t[k][:, r, 128 * c:128 * (c + 1)].bitcast(FP8)
+                        nc.vector.tensor_scalar(
+                            out=dst[:, 32 * q:32 * (q + 1)],
+                            in0=src.rearrange("j (p u e) -> j p u e", u=2, e=2),
+                            scalar1=scl[:, col:col + 1], scalar2=None, op0=MULT)
+
+        def turn_trans(n):
+            words = wide_t.pop(n)[:].bitcast(F32)
+            grp = work.tile([P, 2048], BF16, name="grp", bufs=4, align_bytes=64)
+            t_group[n] = grp
+            banks = []
+            for gi in range(2):
+                tp = psum.tile([P, 512], F32, name="tp")
+                banks.append(tp)
+                for r in range(2):
+                    for u in range(2):
+                        o = 128 * (2 * r + u)
+                        i = 256 * (2 * gi + r) + 128 * u
+                        nc.tensor.transpose(tp[:, o:o + 128], words[:, i:i + 128], ident[:])
+            return banks
+
+        def leave_trans(n, banks):
+            out = t_group[n][:].bitcast(F32)
+            for gi in range(2):
+                nc.scalar.copy(
+                    out=out[:, 512 * gi:512 * (gi + 1)].rearrange("p (j r u) -> p j r u", r=2, u=2),
+                    in_=banks[gi][:].rearrange("p (r u j) -> p j r u", r=2, u=2))
+
+        def turn_alpha(b):
+            words = a_t[b][:].bitcast(F32)
+            grp = work.tile([P, 2048], BF16, name="grp", bufs=4, align_bytes=64)
+            a_group[b] = grp
+            out = grp[:].bitcast(F32)
+            for h in range(2):
+                tp = psum.tile([P, 512], F32, name="tp")
+                for gg in range(2):
+                    g = 2 * h + gg
+                    for u in range(2):
+                        o = 128 * (2 * gg + u)
+                        nc.tensor.transpose(tp[:, o:o + 128], words[:, 256 * g + u:256 * (g + 1):2], ident[:])
+                nc.scalar.copy(
+                    out=out[:, 512 * h:512 * (h + 1)].rearrange("p (g b u) -> p g b u", g=2, u=2),
+                    in_=tp[:].rearrange("p (g u b) -> p g b u", g=2, u=2))
+
+        def quant(grp, codes, scales):
+            nc.vector.quantize_mx(out=codes[:].bitcast(FP8X4), scales=scales[:], in_=grp[:])
+
+        acc_t = {}
+        e_t = {}
+        pf_t = {}
+
+        def multiply(q):
+            k, bp = q // 4, q % 4
+            acc = psum.tile([P, 512], F32, name="acc")
+            acc_t[q] = acc
+            for bi in range(2):
+                b = 2 * bp + bi
+                for g in range(4):
+                    n, gi = 2 * k + g // 2, g % 2
+                    nc.tensor.matmul_mx(
+                        out=acc[:, 256 * bi:256 * (bi + 1)],
+                        lhsT=a_codes[b][:, 128 * g:128 * (g + 1)].bitcast(FP8X4),
+                        lhsT_scale=a_scales[b][:, 128 * g:128 * (g + 1)],
+                        rhs=t_codes[n][:, 256 * gi:256 * (gi + 1)].bitcast(FP8X4),
+                        rhs_scale=t_scales[n][:, 256 * gi:256 * (gi + 1)],
+                        start=(g == 0), stop=(g == 3))
+
+        def expo(q):
+            k, bp = q // 4, q % 4
+            e = work.tile([P, 512], F32, name="e", bufs=3)
+            e_t[q] = e
+            lo = 256 * (k % 4)
+            nc.scalar.activation(
+                out=e[:].rearrange("p (b j) -> p b j", b=2),
+                in_=ll_t[k // 4][bp][:, :, lo:lo + 256], func=EXP)
+
+        def pred(q):
+            k, bp = q // 4, q % 4
+            m = k // 2
+            if k % 2 == 0:
+                pf_t[m, bp] = (work.tile([P, 2, 512], F32, name="pr", bufs=6), work.tile([P, 2, 512], F32, name="fw", bufs=6))
+            lo = 256 * (k % 2)
+            nc.scalar.copy(out=pf_t[m, bp][0][:, :, lo:lo + 256],
+                           in_=acc_t.pop(q)[:].rearrange("p (b j) -> p b j", b=2))
+
+        def store(q):
+            k, bp = q // 4, q % 4
+            m = k // 2
+            lo, hi = (256 * (k % 2), 256 * (k % 2) + 256) if m == 3 else (0, 512)
+            if m < 3 and k % 2 == 0:
+                return
+            for t, o in zip(pf_t[m, bp], out_views):
+                nc.sync.dma_start(out=o[:, 2 * bp:2 * bp + 2, 512 * m + lo:512 * m + hi], in_=t[:, :, lo:hi])
+
+        def forward(q):
+            k, bp = q // 4, q % 4
+            p, f = pf_t[k // 2, bp]
+            lo = 256 * (k % 2)
+            nc.vector.tensor_tensor(
+                out=f[:, :, lo:lo + 256], in0=p[:, :, lo:lo + 256],
+                in1=e_t.pop(q)[:].rearrange("p (b j) -> p b j", b=2), op=MULT)
+
+        pending = None
+        for n in range(19):
+            first, second = 2 * (n - 2) - 1, 2 * (n - 2)
+            if n < N_UNITS:
+                widen(n)
+            if pending is not None:
+                forward(pending)
+                store(pending)
+                pending = None
+            if 1 <= n <= 4:
+                for b in (2 * n - 2, 2 * n - 1):
+                    quant(a_group.pop(b), a_codes[b], a_scales[b])
+            if 0 <= first < N_ITEMS:
+                multiply(first)
+                expo(first)
+                pred(first)
+            banks = turn_trans(n) if n < N_UNITS else None
+            if 0 < second < N_ITEMS:
+                expo(second)
+            if 1 <= n <= N_UNITS:
+                quant(t_group.pop(n - 1), t_codes[n - 1], t_scales[n - 1])
+            if banks is not None:
+                leave_trans(n, banks)
+            if n == 0:
+                expo(0)
+            if n < 4:
+                turn_alpha(2 * n)
+                turn_alpha(2 * n + 1)
+            if 0 <= first < N_ITEMS:
+                forward(first)
+                store(first)
+            if 0 <= second < N_ITEMS:
+                multiply(second)
+                pred(second)
+                pending = second

@@ -18,6 +18,8 @@ EXP = mybir.ActivationFunctionType.Exp
 
 N_UNITS = 16
 N_ITEMS = 32
+FIRST_ITEM = 3.1
+VECTOR_PRED = (26, 28, 30,)
 
 
 def tile_hmm_forward_step_d1_kernel(tc, alpha, trans_bytes, trans_scale, loglik, out_0, out_1):
@@ -51,7 +53,10 @@ def tile_hmm_forward_step_d1_kernel(tc, alpha, trans_bytes, trans_scale, loglik,
         def load_ll(h, bp):
             nc.sync.dma_start(out=ll_t[h][bp][:], in_=loglik_view[:, 2 * bp:2 * bp + 2, 1024 * h:1024 * (h + 1)])
 
-        nc.scalar.dma_start(out=scl[:].rearrange("p (k x) -> p k x", k=8), in_=scale_view)
+        def load_scales(queue, lo, hi):
+            queue.dma_start(out=scl[:, 32 * lo:32 * hi].rearrange("p (k x) -> p k x", k=hi - lo), in_=scale_view[:, lo:hi])
+
+        load_scales(nc.scalar, 0, 1)
         load_bytes(0, 0, 1024)
         load_bytes(0, 1024, 2048)
         load_alpha(0)
@@ -59,6 +64,7 @@ def tile_hmm_forward_step_d1_kernel(tc, alpha, trans_bytes, trans_scale, loglik,
         load_ll(0, 0)
         load_alpha(2)
         load_alpha(3)
+        load_scales(nc.sync, 1, 8)
         load_bytes(1, 0, 2048)
         load_ll(0, 1)
         load_alpha(4)
@@ -78,76 +84,81 @@ def tile_hmm_forward_step_d1_kernel(tc, alpha, trans_bytes, trans_scale, loglik,
         load_bytes(6, 0, 2048)
         load_bytes(7, 0, 2048)
 
-        t_codes = [keep.tile([P, 512], U32, name="tc_%d" % n, align_bytes=64) for n in range(N_UNITS)]
-        t_scales = [keep.tile([P, 512], U8, name="ts_%d" % n, align_bytes=64) for n in range(N_UNITS)]
+        t_codes, t_scales = {}, {}
         a_codes = [keep.tile([P, 512], U32, name="ac_%d" % b, align_bytes=64) for b in range(8)]
         a_scales = [keep.tile([P, 512], U8, name="as_%d" % b, align_bytes=64) for b in range(8)]
 
-        wide_t = {}
-        t_group = {}
-        a_group = {}
+        wide_t, t_group, a_group, banks, acc_t, e_t, pf_t = {}, {}, {}, {}, {}, {}, {}
 
-        def widen(n):
+        dummy = keep.tile([P, 512], BF16, name="dummy")
+        nc.gpsimd.memset(dummy[:], 0.0)
+        warm = psum.tile([P, 512], F32, name="acc")
+
+        def warm_up():
+            nc.tensor.matmul(warm[:], dummy[:, 0:P], dummy[:], start=True, stop=True)
+
+        def widen(n, gi):
             k, gh = n // 2, n % 2
-            w = work.tile([P, 2048], BF16, name="wide", bufs=2, align_bytes=64)
-            wide_t[n] = w
-            for gi in range(2):
-                for r in range(2):
-                    blk = 2 * gi + r
-                    dst = w[:, 512 * blk:512 * (blk + 1)].rearrange("j (u p e) -> j p u e", u=2, e=2)
-                    for q in range(4):
-                        c = 4 * (2 * gh + gi) + q
-                        col = 32 * k + 16 * r + c
-                        src = fp8_t[k][:, r, 128 * c:128 * (c + 1)].bitcast(FP8)
-                        nc.vector.tensor_scalar(
-                            out=dst[:, 32 * q:32 * (q + 1)],
-                            in0=src.rearrange("j (p u e) -> j p u e", u=2, e=2),
-                            scalar1=scl[:, col:col + 1], scalar2=None, op0=MULT)
+            if gi == 0:
+                wide_t[n] = work.tile([P, 2048], BF16, name="wide", bufs=2, align_bytes=64)
+            for r in range(2):
+                blk = 2 * gi + r
+                dst = wide_t[n][:, 512 * blk:512 * (blk + 1)].rearrange("j (u p e) -> j p u e", u=2, e=2)
+                for q in range(4):
+                    c = 4 * (2 * gh + gi) + q
+                    col = 32 * k + 16 * r + c
+                    src = fp8_t[k][:, r, 128 * c:128 * (c + 1)].bitcast(FP8)
+                    nc.vector.tensor_scalar(
+                        out=dst[:, 32 * q:32 * (q + 1)],
+                        in0=src.rearrange("j (p u e) -> j p u e", u=2, e=2),
+                        scalar1=scl[:, col:col + 1], scalar2=None, op0=MULT)
 
-        def turn_trans(n):
-            words = wide_t.pop(n)[:].bitcast(F32)
-            grp = work.tile([P, 2048], BF16, name="grp", bufs=4, align_bytes=64)
-            t_group[n] = grp
-            banks = []
-            for gi in range(2):
-                tp = psum.tile([P, 512], F32, name="tp")
-                banks.append(tp)
-                for r in range(2):
-                    for u in range(2):
-                        o = 128 * (2 * r + u)
-                        i = 256 * (2 * gi + r) + 128 * u
-                        nc.tensor.transpose(tp[:, o:o + 128], words[:, i:i + 128], ident[:])
-            return banks
+        def turn_trans(n, gi):
+            words = wide_t[n][:].bitcast(F32)
+            tp = psum.tile([P, 512], F32, name="tp")
+            banks["t", n, gi] = tp
+            for r in range(2):
+                for u in range(2):
+                    o = 128 * (2 * r + u)
+                    i = 256 * (2 * gi + r) + 128 * u
+                    nc.tensor.transpose(tp[:, o:o + 128], words[:, i:i + 128], ident[:])
 
-        def leave_trans(n, banks):
+        def leave_trans(n, gi):
+            if gi == 0:
+                t_group[n] = work.tile([P, 2048], BF16, name="grp", bufs=5, align_bytes=64)
             out = t_group[n][:].bitcast(F32)
-            for gi in range(2):
-                nc.scalar.copy(
-                    out=out[:, 512 * gi:512 * (gi + 1)].rearrange("p (j r u) -> p j r u", r=2, u=2),
-                    in_=banks[gi][:].rearrange("p (r u j) -> p j r u", r=2, u=2))
+            nc.scalar.copy(
+                out=out[:, 512 * gi:512 * (gi + 1)].rearrange("p (j r u) -> p j r u", r=2, u=2),
+                in_=banks.pop(("t", n, gi))[:].rearrange("p (r u j) -> p j r u", r=2, u=2))
 
-        def turn_alpha(b):
+        def turn_alpha(b, h):
             words = a_t[b][:].bitcast(F32)
-            grp = work.tile([P, 2048], BF16, name="grp", bufs=4, align_bytes=64)
-            a_group[b] = grp
-            out = grp[:].bitcast(F32)
-            for h in range(2):
-                tp = psum.tile([P, 512], F32, name="tp")
-                for gg in range(2):
-                    g = 2 * h + gg
-                    for u in range(2):
-                        o = 128 * (2 * gg + u)
-                        nc.tensor.transpose(tp[:, o:o + 128], words[:, 256 * g + u:256 * (g + 1):2], ident[:])
-                nc.scalar.copy(
-                    out=out[:, 512 * h:512 * (h + 1)].rearrange("p (g b u) -> p g b u", g=2, u=2),
-                    in_=tp[:].rearrange("p (g u b) -> p g b u", g=2, u=2))
+            tp = psum.tile([P, 512], F32, name="tp")
+            banks["a", b, h] = tp
+            for gg in range(2):
+                g = 2 * h + gg
+                for u in range(2):
+                    o = 128 * (2 * gg + u)
+                    nc.tensor.transpose(tp[:, o:o + 128], words[:, 256 * g + u:256 * (g + 1):2], ident[:])
+
+        def leave_alpha(b, h):
+            if h == 0:
+                a_group[b] = work.tile([P, 2048], BF16, name="grp", bufs=5, align_bytes=64)
+            out = a_group[b][:].bitcast(F32)
+            nc.scalar.copy(
+                out=out[:, 512 * h:512 * (h + 1)].rearrange("p (g b u) -> p g b u", g=2, u=2),
+                in_=banks.pop(("a", b, h))[:].rearrange("p (g u b) -> p g b u", g=2, u=2))
 
         def quant(grp, codes, scales):
             nc.vector.quantize_mx(out=codes[:].bitcast(FP8X4), scales=scales[:], in_=grp[:])
 
-        acc_t = {}
-        e_t = {}
-        pf_t = {}
+        def quant_trans(n):
+            t_codes[n] = work.tile([P, 512], U32, name="tc", bufs=8, align_bytes=64)
+            t_scales[n] = work.tile([P, 512], U8, name="ts", bufs=8, align_bytes=64)
+            quant(t_group.pop(n), t_codes[n], t_scales[n])
+
+        def quant_alpha(b):
+            quant(a_group.pop(b), a_codes[b], a_scales[b])
 
         def multiply(q):
             k, bp = q // 4, q % 4
@@ -167,7 +178,7 @@ def tile_hmm_forward_step_d1_kernel(tc, alpha, trans_bytes, trans_scale, loglik,
 
         def expo(q):
             k, bp = q // 4, q % 4
-            e = work.tile([P, 512], F32, name="e", bufs=3)
+            e = work.tile([P, 512], F32, name="e", bufs=4)
             e_t[q] = e
             lo = 256 * (k % 4)
             nc.scalar.activation(
@@ -180,58 +191,50 @@ def tile_hmm_forward_step_d1_kernel(tc, alpha, trans_bytes, trans_scale, loglik,
             if k % 2 == 0:
                 pf_t[m, bp] = (work.tile([P, 2, 512], F32, name="pr", bufs=6), work.tile([P, 2, 512], F32, name="fw", bufs=6))
             lo = 256 * (k % 2)
-            nc.scalar.copy(out=pf_t[m, bp][0][:, :, lo:lo + 256],
-                           in_=acc_t.pop(q)[:].rearrange("p (b j) -> p b j", b=2))
-
-        def store(q):
-            k, bp = q // 4, q % 4
-            m = k // 2
-            lo, hi = (256 * (k % 2), 256 * (k % 2) + 256) if m == 3 else (0, 512)
-            if m < 3 and k % 2 == 0:
-                return
-            for t, o in zip(pf_t[m, bp], out_views):
-                nc.sync.dma_start(out=o[:, 2 * bp:2 * bp + 2, 512 * m + lo:512 * m + hi], in_=t[:, :, lo:hi])
+            copy = nc.vector.tensor_copy if q in VECTOR_PRED else nc.scalar.copy
+            copy(out=pf_t[m, bp][0][:, :, lo:lo + 256],
+                 in_=acc_t.pop(q)[:].rearrange("p (b j) -> p b j", b=2))
 
         def forward(q):
             k, bp = q // 4, q % 4
-            p, f = pf_t[k // 2, bp]
+            m = k // 2
+            p, f = pf_t[m, bp]
             lo = 256 * (k % 2)
             nc.vector.tensor_tensor(
                 out=f[:, :, lo:lo + 256], in0=p[:, :, lo:lo + 256],
                 in1=e_t.pop(q)[:].rearrange("p (b j) -> p b j", b=2), op=MULT)
+            if m == 3:
+                a, b = lo, lo + 256
+            elif k % 2 == 1:
+                a, b = 0, 512
+            else:
+                return
+            for t, o in zip(pf_t[m, bp], out_views):
+                nc.sync.dma_start(out=o[:, 2 * bp:2 * bp + 2, 512 * m + a:512 * m + b], in_=t[:, :, a:b])
 
-        pending = None
-        for n in range(19):
-            first, second = 2 * (n - 2) - 1, 2 * (n - 2)
-            if n < N_UNITS:
-                widen(n)
-            if pending is not None:
-                forward(pending)
-                store(pending)
-                pending = None
-            if 1 <= n <= 4:
-                for b in (2 * n - 2, 2 * n - 1):
-                    quant(a_group.pop(b), a_codes[b], a_scales[b])
-            if 0 <= first < N_ITEMS:
-                multiply(first)
-                expo(first)
-                pred(first)
-            banks = turn_trans(n) if n < N_UNITS else None
-            if 0 < second < N_ITEMS:
-                expo(second)
-            if 1 <= n <= N_UNITS:
-                quant(t_group.pop(n - 1), t_codes[n - 1], t_scales[n - 1])
-            if banks is not None:
-                leave_trans(n, banks)
-            if n == 0:
-                expo(0)
-            if n < 4:
-                turn_alpha(2 * n)
-                turn_alpha(2 * n + 1)
-            if 0 <= first < N_ITEMS:
-                forward(first)
-                store(first)
-            if 0 <= second < N_ITEMS:
-                multiply(second)
-                pred(second)
-                pending = second
+        steps = []
+        for n in range(N_UNITS):
+            for h in range(2):
+                steps.append((n + 0.2 * h, widen, (n, h)))
+                steps.append((n + 0.30 + 0.05 * h, turn_trans, (n, h)))
+                steps.append((n + 0.65 + 0.05 * h, leave_trans, (n, h)))
+            steps.append((n + 1.35, quant_trans, (n,)))
+        for b in range(8):
+            a = 0.45 + 0.5 * b
+            for h in range(2):
+                steps.append((a + 0.1 * h, turn_alpha, (b, h)))
+                steps.append((a + 0.3 + 0.1 * h, leave_alpha, (b, h)))
+            steps.append((a + 0.6, quant_alpha, (b,)))
+        for q in range(N_ITEMS):
+            i = FIRST_ITEM + 0.5 * q
+            steps.append((i, multiply, (q,)))
+            steps.append((i + 0.2, expo, (q,)))
+            steps.append((i + 0.35, pred, (q,)))
+            steps.append((i + 0.85, forward, (q,)))
+
+        for i in range(8):
+            warm_up()
+        for pos, step, args in sorted(steps, key=lambda x: x[0]):
+            if pos < FIRST_ITEM and step in (turn_trans, turn_alpha):
+                warm_up()
+            step(*args)

from contextlib import ExitStack

import concourse.mybir as mybir
from concourse.masks import make_identity

B, S = 1024, 2048
P = 128
FLOPS = 2 * B * S * S

F32 = mybir.dt.float32
BF16 = mybir.dt.bfloat16
U32 = mybir.dt.uint32
U8 = mybir.dt.uint8
FP8 = mybir.dt.float8_e4m3fn
FP8X4 = mybir.dt.float8_e4m3fn_x4
MULT = mybir.AluOpType.mult
EXP = mybir.ActivationFunctionType.Exp

N_UNITS = 16
N_ITEMS = 32
FIRST_ITEM = 3.1
VECTOR_PRED = (26, 28, 30,)


def tile_hmm_forward_step_d1_kernel(tc, alpha, trans_bytes, trans_scale, loglik, out_0, out_1):
    nc = tc.nc
    bytes_view = trans_bytes.rearrange("(k p r) s -> k p r s", p=P, r=2)
    scale_view = trans_scale.rearrange("(k p r) c -> p k (r c)", p=P, r=2)
    loglik_view = loglik.rearrange("(b p) j -> p b j", p=P)
    out_views = [o.rearrange("(b p) j -> p b j", p=P) for o in (out_0, out_1)]

    with ExitStack() as ctx:
        keep = ctx.enter_context(tc.tile_pool(name="keep", bufs=1))
        work = ctx.enter_context(tc.tile_pool(name="work", bufs=3))
        psum = ctx.enter_context(tc.psum_pool(name="psum", bufs=4))

        ident = keep.tile([P, P], F32, name="ident")
        make_identity(nc, ident[:])

        ctx.enter_context(tc.manual_schedule())

        scl = keep.tile([P, 256], F32, name="scl")
        fp8_t = [keep.tile([P, 2, S], U8, name="fp8_%d" % k) for k in range(8)]
        a_t = [keep.tile([P, S], BF16, name="a_%d" % b) for b in range(8)]
        ll_t = [[keep.tile([P, 2, 1024], BF16, name="ll_%d_%d" % (h, bp)) for bp in range(4)] for h in range(2)]

        def load_bytes(k, lo, hi):
            nc.sync.dma_start(out=fp8_t[k][:, :, lo:hi], in_=bytes_view[k][:, :, lo:hi])

        def load_alpha(b):
            nc.sync.dma_start(out=a_t[b][:], in_=alpha[b * P:(b + 1) * P, :])

        def load_ll(h, bp):
            nc.sync.dma_start(out=ll_t[h][bp][:], in_=loglik_view[:, 2 * bp:2 * bp + 2, 1024 * h:1024 * (h + 1)])

        def load_scales(queue, lo, hi):
            queue.dma_start(out=scl[:, 32 * lo:32 * hi].rearrange("p (k x) -> p k x", k=hi - lo), in_=scale_view[:, lo:hi])

        load_scales(nc.scalar, 0, 1)
        load_bytes(0, 0, 1024)
        load_bytes(0, 1024, 2048)
        load_alpha(0)
        load_alpha(1)
        load_ll(0, 0)
        load_alpha(2)
        load_alpha(3)
        load_scales(nc.sync, 1, 8)
        load_bytes(1, 0, 2048)
        load_ll(0, 1)
        load_alpha(4)
        load_alpha(5)
        load_ll(0, 2)
        load_alpha(6)
        load_alpha(7)
        load_bytes(2, 0, 2048)
        load_ll(0, 3)
        load_bytes(3, 0, 2048)
        load_bytes(4, 0, 2048)
        load_ll(1, 0)
        load_ll(1, 1)
        load_bytes(5, 0, 2048)
        load_ll(1, 2)
        load_ll(1, 3)
        load_bytes(6, 0, 2048)
        load_bytes(7, 0, 2048)

        t_codes, t_scales = {}, {}
        a_codes = [keep.tile([P, 512], U32, name="ac_%d" % b, align_bytes=64) for b in range(8)]
        a_scales = [keep.tile([P, 512], U8, name="as_%d" % b, align_bytes=64) for b in range(8)]

        wide_t, t_group, a_group, banks, acc_t, e_t, pf_t = {}, {}, {}, {}, {}, {}, {}

        dummy = keep.tile([P, 512], BF16, name="dummy")
        nc.gpsimd.memset(dummy[:], 0.0)
        warm = psum.tile([P, 512], F32, name="acc")

        def warm_up():
            nc.tensor.matmul(warm[:], dummy[:, 0:P], dummy[:], start=True, stop=True)

        def widen(n, gi):
            k, gh = n // 2, n % 2
            if gi == 0:
                wide_t[n] = work.tile([P, 2048], BF16, name="wide", bufs=2, align_bytes=64)
            for r in range(2):
                blk = 2 * gi + r
                dst = wide_t[n][:, 512 * blk:512 * (blk + 1)].rearrange("j (u p e) -> j p u e", u=2, e=2)
                for q in range(4):
                    c = 4 * (2 * gh + gi) + q
                    col = 32 * k + 16 * r + c
                    src = fp8_t[k][:, r, 128 * c:128 * (c + 1)].bitcast(FP8)
                    nc.vector.tensor_scalar(
                        out=dst[:, 32 * q:32 * (q + 1)],
                        in0=src.rearrange("j (p u e) -> j p u e", u=2, e=2),
                        scalar1=scl[:, col:col + 1], scalar2=None, op0=MULT)

        def turn_trans(n, gi):
            words = wide_t[n][:].bitcast(F32)
            tp = psum.tile([P, 512], F32, name="tp")
            banks["t", n, gi] = tp
            for r in range(2):
                for u in range(2):
                    o = 128 * (2 * r + u)
                    i = 256 * (2 * gi + r) + 128 * u
                    nc.tensor.transpose(tp[:, o:o + 128], words[:, i:i + 128], ident[:])

        def leave_trans(n, gi):
            if gi == 0:
                t_group[n] = work.tile([P, 2048], BF16, name="grp", bufs=5, align_bytes=64)
            out = t_group[n][:].bitcast(F32)
            nc.scalar.copy(
                out=out[:, 512 * gi:512 * (gi + 1)].rearrange("p (j r u) -> p j r u", r=2, u=2),
                in_=banks.pop(("t", n, gi))[:].rearrange("p (r u j) -> p j r u", r=2, u=2))

        def turn_alpha(b, h):
            words = a_t[b][:].bitcast(F32)
            tp = psum.tile([P, 512], F32, name="tp")
            banks["a", b, h] = tp
            for gg in range(2):
                g = 2 * h + gg
                for u in range(2):
                    o = 128 * (2 * gg + u)
                    nc.tensor.transpose(tp[:, o:o + 128], words[:, 256 * g + u:256 * (g + 1):2], ident[:])

        def leave_alpha(b, h):
            if h == 0:
                a_group[b] = work.tile([P, 2048], BF16, name="grp", bufs=5, align_bytes=64)
            out = a_group[b][:].bitcast(F32)
            nc.scalar.copy(
                out=out[:, 512 * h:512 * (h + 1)].rearrange("p (g b u) -> p g b u", g=2, u=2),
                in_=banks.pop(("a", b, h))[:].rearrange("p (g u b) -> p g b u", g=2, u=2))

        def quant(grp, codes, scales):
            nc.vector.quantize_mx(out=codes[:].bitcast(FP8X4), scales=scales[:], in_=grp[:])

        def quant_trans(n):
            t_codes[n] = work.tile([P, 512], U32, name="tc", bufs=8, align_bytes=64)
            t_scales[n] = work.tile([P, 512], U8, name="ts", bufs=8, align_bytes=64)
            quant(t_group.pop(n), t_codes[n], t_scales[n])

        def quant_alpha(b):
            quant(a_group.pop(b), a_codes[b], a_scales[b])

        def multiply(q):
            k, bp = q // 4, q % 4
            acc = psum.tile([P, 512], F32, name="acc")
            acc_t[q] = acc
            for bi in range(2):
                b = 2 * bp + bi
                for g in range(4):
                    n, gi = 2 * k + g // 2, g % 2
                    nc.tensor.matmul_mx(
                        out=acc[:, 256 * bi:256 * (bi + 1)],
                        lhsT=a_codes[b][:, 128 * g:128 * (g + 1)].bitcast(FP8X4),
                        lhsT_scale=a_scales[b][:, 128 * g:128 * (g + 1)],
                        rhs=t_codes[n][:, 256 * gi:256 * (gi + 1)].bitcast(FP8X4),
                        rhs_scale=t_scales[n][:, 256 * gi:256 * (gi + 1)],
                        start=(g == 0), stop=(g == 3))

        def expo(q):
            k, bp = q // 4, q % 4
            e = work.tile([P, 512], F32, name="e", bufs=4)
            e_t[q] = e
            lo = 256 * (k % 4)
            nc.scalar.activation(
                out=e[:].rearrange("p (b j) -> p b j", b=2),
                in_=ll_t[k // 4][bp][:, :, lo:lo + 256], func=EXP)

        def pred(q):
            k, bp = q // 4, q % 4
            m = k // 2
            if k % 2 == 0:
                pf_t[m, bp] = (work.tile([P, 2, 512], F32, name="pr", bufs=6), work.tile([P, 2, 512], F32, name="fw", bufs=6))
            lo = 256 * (k % 2)
            copy = nc.vector.tensor_copy if q in VECTOR_PRED else nc.scalar.copy
            copy(out=pf_t[m, bp][0][:, :, lo:lo + 256],
                 in_=acc_t.pop(q)[:].rearrange("p (b j) -> p b j", b=2))

        def forward(q):
            k, bp = q // 4, q % 4
            m = k // 2
            p, f = pf_t[m, bp]
            lo = 256 * (k % 2)
            nc.vector.tensor_tensor(
                out=f[:, :, lo:lo + 256], in0=p[:, :, lo:lo + 256],
                in1=e_t.pop(q)[:].rearrange("p (b j) -> p b j", b=2), op=MULT)
            if m == 3:
                a, b = lo, lo + 256
            elif k % 2 == 1:
                a, b = 0, 512
            else:
                return
            for t, o in zip(pf_t[m, bp], out_views):
                nc.sync.dma_start(out=o[:, 2 * bp:2 * bp + 2, 512 * m + a:512 * m + b], in_=t[:, :, a:b])

        steps = []
        for n in range(N_UNITS):
            for h in range(2):
                steps.append((n + 0.2 * h, widen, (n, h)))
                steps.append((n + 0.30 + 0.05 * h, turn_trans, (n, h)))
                steps.append((n + 0.65 + 0.05 * h, leave_trans, (n, h)))
            steps.append((n + 1.35, quant_trans, (n,)))
        for b in range(8):
            a = 0.45 + 0.5 * b
            for h in range(2):
                steps.append((a + 0.1 * h, turn_alpha, (b, h)))
                steps.append((a + 0.3 + 0.1 * h, leave_alpha, (b, h)))
            steps.append((a + 0.6, quant_alpha, (b,)))
        for q in range(N_ITEMS):
            i = FIRST_ITEM + 0.5 * q
            steps.append((i, multiply, (q,)))
            steps.append((i + 0.2, expo, (q,)))
            steps.append((i + 0.35, pred, (q,)))
            steps.append((i + 0.85, forward, (q,)))

        for i in range(8):
            warm_up()
        for pos, step, args in sorted(steps, key=lambda x: x[0]):
            if pos < FIRST_ITEM and step in (turn_trans, turn_alpha):
                warm_up()
            step(*args)
